import numpy as np
import ml_dtypes


def mxq(x, axis, fmt="e4m3"):
    dtype, down = {"e4m3": (ml_dtypes.float8_e4m3fn, 7), "e5m2": (ml_dtypes.float8_e5m2, 14)}[fmt]
    v = np.moveaxis(np.asarray(x, np.float32).astype(ml_dtypes.bfloat16).astype(np.float64), axis, -1)
    blocks = v.reshape(v.shape[:-1] + (-1, 32))
    amax = np.abs(blocks).max(-1, keepdims=True)
    byte = np.maximum(np.where(amax > 0, np.frexp(amax)[1] - 1 + 127, 0) - down, 1)
    scale = np.exp2(byte - 127.0)
    codes = (blocks / scale).astype(np.float32).astype(dtype).astype(np.float64)
    return np.moveaxis((codes * scale).reshape(v.shape), -1, axis)


WIDE = False


def mx_kscale(k):
    if not WIDE:
        return np.ones(k)
    levels = np.array([24, -24, 12, -12, 0])
    if k % 512:
        return np.exp2(np.random.permutation(np.resize(levels, k // 32))).repeat(32)
    a = np.empty((k // 512, 16))
    for p in range(k // 512):
        a[p, :8] = np.random.permutation(np.resize(levels, 8))
        for g in range(8):
            far = levels[np.abs(levels - a[p, g]) >= 10]
            a[p, g + 8] = far[np.random.randint(len(far))]
    return np.exp2(a.ravel()).repeat(32)


def f64(x):
    return np.asarray(x).astype(np.float64)


def striped(idx):
    return np.tile(idx.reshape(-1, 16).T, (8, 1)).astype(np.uint16)


def unstriped(offs):
    return offs[:16].T.reshape(-1).astype(np.int64)


E2M1 = np.array([0.0, 0.5, 1.0, 1.5, 2.0, 3.0, 4.0, 6.0, -0.0, -0.5, -1.0, -1.5, -2.0, -3.0, -4.0, -6.0])


def pack_weight(w, fmt):
    k, n = w.shape
    w = f64(np.asarray(w, np.float32).astype(ml_dtypes.bfloat16)).reshape(k // 32, 32, n)
    amax = np.abs(w).max(1)
    if fmt == "e4m3":
        byte = np.frexp(amax)[1] - 1 + 127 - 7
    else:
        mant, ex = np.frexp(amax / 6.0)
        byte = np.where(mant > 0.5, ex, ex - 1) + 127
    byte = np.clip(np.where(amax > 0, byte, 1), 1, 254)
    scaled = (w * np.exp2(127.0 - byte)[:, None, :]).reshape(k, n).astype(np.float32)
    by_word = np.ascontiguousarray(scaled.reshape(k // 512, 128, 4, n).transpose(0, 1, 3, 2))
    if fmt == "e4m3":
        words = by_word.astype(ml_dtypes.float8_e4m3fn).view(np.uint8)
    else:
        c = by_word.astype(ml_dtypes.float4_e2m1fn).view(np.uint8) & 0xF
        words = (c[..., 0::2] | (c[..., 1::2] << 4)).reshape(k // 512, 128, 2 * n)
    return np.ascontiguousarray(words), np.ascontiguousarray(byte.astype(np.uint8).reshape(k // 512, 16, n))


def unpack_weight(words, scales, fmt):
    g, _, n = scales.shape
    words = np.ascontiguousarray(words).reshape(g, 128, n, -1)
    if fmt == "e4m3":
        vals = words.view(ml_dtypes.float8_e4m3fn).astype(np.float64)
    else:
        nib = np.empty((g, 128, n, 4), np.uint8)
        nib[..., 0::2] = words & 0xF
        nib[..., 1::2] = words >> 4
        vals = E2M1[nib]
    vals = vals * np.repeat(np.exp2(scales.astype(np.float64) - 127.0), 8, axis=1)[..., None]
    return vals.transpose(0, 1, 3, 2).reshape(g * 512, n)


def pack_table4(v):
    words, scales = pack_weight(v, "e2m1")
    g, t = words.shape[0] // 2, v.shape[1]
    return np.ascontiguousarray(words.reshape(g, 2, 128, t, 2).transpose(0, 2, 3, 1, 4).reshape(g, 128, t, 4)), scales


def unpack_table4(words, scales):
    g, _, t, _ = words.shape
    return unpack_weight(words.reshape(g, 128, t, 2, 2).transpose(0, 3, 1, 2, 4).reshape(2 * g, 128, 2 * t), scales, "e2m1")


def sigm(f):
    return 1.0 / (1.0 + np.exp(-np.maximum(f, -700.0)))


K, M, N, T, J = 512, 1024, 1024, 2048, 1024


def setup_inputs():
    n = np.random.standard_normal
    s = mx_kscale(K)[:, None]
    s2 = mx_kscale(M)[:, None]
    h = np.tanh(n((N, T)))
    p_tab = pack_table4(h * s2)
    p_wz = pack_weight(n((K, N)) / np.sqrt(K) / s, "e4m3")
    p_uz = pack_weight(n((M, N)) / np.sqrt(M) / s2, "e2m1")
    p_wn = pack_weight(n((K, N)) / np.sqrt(K) / s, "e4m3")
    p_un = pack_weight(n((M, N)) / np.sqrt(M) / s2, "e2m1")
    return {
        "x": (n((K, J)) * s).astype(np.float32),
        "tab_words": p_tab[0],
        "tab_scales": p_tab[1],
        "wz_words": p_wz[0],
        "wz_scales": p_wz[1],
        "uz_words": p_uz[0],
        "uz_scales": p_uz[1],
        "wn_words": p_wn[0],
        "wn_scales": p_wn[1],
        "un_words": p_un[0],
        "un_scales": p_un[1],
        "bz": (0.3 * n(N)).astype(np.float32),
        "bn": (0.3 * n(N)).astype(np.float32),
        "hT": (h).astype(np.float32),
        "wgo": np.tile(np.random.uniform(0.5, 2.0, J), (128, 1)).astype(np.float32),
        "offs": striped(np.random.permutation(T)[:J]),
    }


def reference(x, tab_words, tab_scales, wz_words, wz_scales, uz_words, uz_scales, wn_words, wn_scales, un_words, un_scales, bz, bn, hT, wgo, offs):
    idx = unstriped(offs)
    x_ = mxq(f64(x), 0, "e4m3")
    tab_ = unpack_table4(tab_words, tab_scales)[:, idx]
    wz_ = unpack_weight(wz_words, wz_scales, "e4m3")
    uz_ = unpack_weight(uz_words, uz_scales, "e2m1")
    wn_ = unpack_weight(wn_words, wn_scales, "e4m3")
    un_ = unpack_weight(un_words, un_scales, "e2m1")
    sz = wz_.T @ x_ + uz_.T @ tab_
    z = sigm(sz + f64(bz)[:, None])
    xn = wn_.T @ x_
    hn = un_.T @ tab_
    cd = np.tanh(xn + f64(bn)[:, None] + z * hn)
    out = np.zeros((N, T))
    out[:, idx] = f64(wgo)[0] * (f64(hT)[:, idx] + z * (cd - f64(hT)[:, idx]))
    return out

@@ -1,0 +1,186 @@
+from contextlib import ExitStack
+
+import concourse.mybir as mybir
+from concourse.masks import make_identity
+
+K, M, N, T, J = 512, 1024, 1024, 2048, 1024
+FLOPS = 2 * J * N * (2 * K + 2 * M)
+
+F32 = mybir.dt.float32
+BF16 = mybir.dt.bfloat16
+I32 = mybir.dt.int32
+U32 = mybir.dt.uint32
+U16 = mybir.dt.uint16
+U8 = mybir.dt.uint8
+FP8X4 = mybir.dt.float8_e4m3fn_x4
+FP4X4 = mybir.dt.float4_e2m1fn_x4
+ACT = mybir.ActivationFunctionType
+ALU = mybir.AluOpType
+
+P = 128
+HALF = 512
+HALVES = J // HALF
+TILES = N // P
+WINDOWS = 3
+
+
+def load_scale_rows(queue, planes, scales):
+    for q in range(4):
+        queue.dma_start(
+            out=planes[32 * q : 32 * q + 4, :, :],
+            in_=scales[:, 4 * q : 4 * q + 4, :].rearrange("a r n -> r a n").bitcast(I32),
+        )
+
+
+def tile_list_tgn_mgu_kernel(
+    tc, x, tab_words, tab_scales, wz_words, wz_scales, uz_words, uz_scales,
+    wn_words, wn_scales, un_words, un_scales, bz, bn, hT, wgo, offs, out,
+):
+    nc = tc.nc
+    with ExitStack() as ctx:
+        keep = ctx.enter_context(tc.tile_pool(name="keep", bufs=1))
+        hpool = ctx.enter_context(tc.tile_pool(name="hpool", bufs=4))
+        work = ctx.enter_context(tc.tile_pool(name="work", bufs=2))
+        psum = ctx.enter_context(tc.psum_pool(name="psum", bufs=1))
+
+        offsets = keep.tile([P, J // 16], U16, name="offsets")
+        nc.sync.dma_start(offsets[:], offs)
+
+        tab_planes = keep.tile([P, 2, T // 4], I32, name="tab_planes", align_bytes=64)
+        w_planes = keep.tile([P, 6, N // 4], I32, name="w_planes", align_bytes=64)
+        vec_rows = keep.tile([P, P], F32, name="vec_rows")
+        nc.vector.memset(tab_planes[:], 0)
+        nc.vector.memset(w_planes[:], 0)
+        nc.vector.memset(vec_rows[:], 0.0)
+
+        table = keep.tile([P, T], I32, name="table", align_bytes=64)
+        nc.sync.dma_start(out=table[:], in_=tab_words[0].rearrange("p t b -> p (t b)").bitcast(I32))
+        load_scale_rows(nc.sync, tab_planes, tab_scales)
+
+        x_raw = [keep.tile([P, 4, HALF], F32, name=f"x_raw{h}") for h in range(HALVES)]
+        x_rows = x.rearrange("(p i) j -> p i j", i=4)
+        nc.sync.dma_start(out=x_raw[0][:], in_=x_rows[:, :, 0:HALF])
+
+        load_scale_rows(nc.scalar, w_planes[:, 0:1, :], wz_scales)
+        load_scale_rows(nc.scalar, w_planes[:, 1:3, :], uz_scales)
+        load_scale_rows(nc.scalar, w_planes[:, 3:4, :], wn_scales)
+        load_scale_rows(nc.scalar, w_planes[:, 4:6, :], un_scales)
+        nc.scalar.dma_start(out=vec_rows[0:TILES, :], in_=bz.rearrange("(c p) -> c p", p=P))
+        nc.scalar.dma_start(out=vec_rows[TILES : 2 * TILES, :], in_=bn.rearrange("(c p) -> c p", p=P))
+
+        wz = keep.tile([P, N], I32, name="wz", align_bytes=64)
+        wn = keep.tile([P, N], I32, name="wn", align_bytes=64)
+        uz = keep.tile([P, 2, N // 2], I32, name="uz", align_bytes=64)
+        un = keep.tile([P, 2, N // 2], I32, name="un", align_bytes=64)
+        nc.sync.dma_start(out=wz[:], in_=wz_words[0].rearrange("p n b -> p (n b)").bitcast(I32))
+        nc.sync.dma_start(out=uz[:], in_=uz_words.rearrange("a p n -> p a n").bitcast(I32))
+        nc.sync.dma_start(out=un[:], in_=un_words.rearrange("a p n -> p a n").bitcast(I32))
+        nc.sync.dma_start(out=wn[:], in_=wn_words[0].rearrange("p n b -> p (n b)").bitcast(I32))
+        nc.sync.dma_start(out=x_raw[1][:], in_=x_rows[:, :, HALF:J])
+        weight = keep.tile([P, J], F32, name="weight")
+
+        windows = [keep.tile([P, T], F32, name=f"window{i}") for i in range(WINDOWS)]
+        for win in windows:
+            nc.vector.memset(win[:], 0.0)
+
+        ident = keep.tile([P, P], F32, name="ident")
+        make_identity(nc, ident[:])
+        vec_ps = psum.tile([P, P], F32, name="vec_ps", tag="sz0")
+        nc.tensor.transpose(vec_ps[:], vec_rows[:], ident[:])
+        bias = keep.tile([P, 2 * TILES], F32, name="bias")
+        nc.scalar.copy(out=bias[:], in_=vec_ps[:, 0 : 2 * TILES])
+
+        picked = keep.tile([P, J], U32, name="picked", align_bytes=64)
+        v_codes = keep.tile([P, HALVES, 2, 2 * HALF], U8, name="v_codes", align_bytes=64)
+        v_scales = keep.tile([P, HALVES, 2, HALF], U8, name="v_scales", align_bytes=64)
+        x_bf = keep.tile([P, HALVES, HALF, 4], BF16, name="x_bf", align_bytes=64)
+        x_codes = keep.tile([P, J], U32, name="x_codes", align_bytes=64)
+        x_scales = keep.tile([P, J], U8, name="x_scales", align_bytes=64)
+        for h in range(HALVES):
+            cols = slice(h * HALF, (h + 1) * HALF)
+            part = offsets[:, h * HALF // 16 : (h + 1) * HALF // 16]
+            nc.scalar.copy(out=x_bf[:, h, :, :], in_=x_raw[h][:].rearrange("p i j -> p j i"))
+            nc.vector.tensor_copy(out=picked[:, cols], in_=table[:].bitcast(U32).indirect(part))
+            for a in range(2):
+                nc.vector.tensor_copy(
+                    out=v_scales[:, h, a, :], in_=tab_planes[:, a, :].bitcast(U8).indirect(part)
+                )
+            nc.vector.tensor_copy(
+                out=v_codes[:, h, :, :].bitcast(U16),
+                in_=picked[:, cols].bitcast(U16).rearrange("p (j d) -> p d j", d=2),
+            )
+            nc.vector.quantize_mx(
+                out=x_codes[:, cols].bitcast(FP8X4),
+                scales=x_scales[:, cols],
+                in_=x_bf[:, h, :, :].rearrange("p j i -> p (j i)"),
+            )
+
+        w_scale = w_planes[:].bitcast(U8)
+
+        def x_pass(bank, words, plane, c, h, start, stop):
+            nc.tensor.matmul_mx(
+                out=bank[:],
+                lhsT=words[:, c * P : (c + 1) * P].bitcast(FP8X4),
+                lhsT_scale=w_scale[:, plane, c * P : (c + 1) * P],
+                rhs=x_codes[:, h * HALF : (h + 1) * HALF].bitcast(FP8X4),
+                rhs_scale=x_scales[:, h * HALF : (h + 1) * HALF],
+                start=start,
+                stop=stop,
+            )
+
+        def v_pass(bank, words, plane, a, c, h, start, stop):
+            nc.tensor.matmul_mx(
+                out=bank[:],
+                lhsT=words[:, a, :].bitcast(U8)[:, 2 * c * P : 2 * (c + 1) * P].bitcast(FP4X4),
+                lhsT_scale=w_scale[:, plane + a, c * P : (c + 1) * P],
+                rhs=v_codes[:, h, a, :].bitcast(FP4X4),
+                rhs_scale=v_scales[:, h, a, :],
+                start=start,
+                stop=stop,
+            )
+
+        for c in range(TILES):
+            rows = slice(c * P, (c + 1) * P)
+            h_all = hpool.tile([P, T], F32, name="h_all")
+            nc.sync.dma_start(out=h_all[:], in_=hT[rows, :])
+            if c == 0:
+                nc.sync.dma_start(out=weight[:], in_=wgo)
+
+            z = work.tile([P, J], F32, name="z", bufs=3)
+            u = work.tile([P, J], F32, name="u")
+            t = work.tile([P, J], F32, name="t")
+            cd = work.tile([P, J], F32, name="cd")
+            xn = []
+            for h in range(HALVES):
+                cols = slice(h * HALF, (h + 1) * HALF)
+                unit = HALVES * c + h
+                sz = psum.tile([P, HALF], F32, name="sz", tag=f"sz{unit % 2}")
+                v_pass(sz, uz, 1, 0, c, h, True, False)
+                v_pass(sz, uz, 1, 1, c, h, False, False)
+                x_pass(sz, wz, 0, c, h, False, True)
+                hn = psum.tile([P, HALF], F32, name="hn", tag=f"hn{unit % 3}")
+                v_pass(hn, un, 4, 0, c, h, True, False)
+                v_pass(hn, un, 4, 1, c, h, False, True)
+                xb = psum.tile([P, HALF], F32, name="xb", tag=f"xn{unit % 3}")
+                x_pass(xb, wn, 3, c, h, True, True)
+                xn.append(xb)
+                nc.scalar.activation(out=z[:, cols], in_=sz[:], func=ACT.Sigmoid, bias=bias[:, c : c + 1])
+                nc.vector.tensor_tensor(out=u[:, cols], in0=z[:, cols], in1=hn[:], op=ALU.mult)
+            for h in range(HALVES):
+                cols = slice(h * HALF, (h + 1) * HALF)
+                nc.vector.tensor_tensor(out=t[:, cols], in0=u[:, cols], in1=xn[h][:], op=ALU.add)
+            nc.scalar.activation(out=cd[:], in_=t[:], func=ACT.Tanh, bias=bias[:, TILES + c : TILES + c + 1])
+
+            hg = work.tile([P, J], F32, name="hg", bufs=6)
+            nc.vector.tensor_copy(out=hg[:], in_=h_all[:].indirect(offsets[:]))
+            d = work.tile([P, J], F32, name="d")
+            e = work.tile([P, J], F32, name="e")
+            r = work.tile([P, J], F32, name="r")
+            rw = work.tile([P, J], F32, name="rw")
+            nc.gpsimd.tensor_tensor(out=d[:], in0=cd[:], in1=hg[:], op=ALU.subtract)
+            nc.gpsimd.tensor_tensor(out=e[:], in0=d[:], in1=z[:], op=ALU.mult)
+            nc.gpsimd.tensor_tensor(out=r[:], in0=e[:], in1=hg[:], op=ALU.add)
+            nc.gpsimd.tensor_tensor(out=rw[:], in0=r[:], in1=weight[:], op=ALU.mult)
+            win = windows[c % WINDOWS]
+            nc.vector.tensor_copy(out=win[:].indirect(offsets[:]), in_=rw[:])
+            nc.sync.dma_start(out=out[rows, :], in_=win[:])

@@ -21,7 +21,33 @@ P = 128
 HALF = 512
 HALVES = J // HALF
 TILES = N // P
-WINDOWS = 3
+WINDOWS = 2
+U_ON_GPSIMD = (5, 6, 7)
+LOADS = ("bias", "tabs", "table", "x0", "uzs", "wzs", "uns", "wns", "x1", "h0", "z0", "n0", "h1", "h2", "z1", "n1", "z2", "n2", "w", "h3", "h4", "h5", "h6", "h7", "W")
+CHUNKS = (0, 2, 8, 8)
+SPLIT_MUL = (0, 7)
+T_ON_V = (0, 1, 2, 3, 4)
+DE_ON_V = ()
+FINAL = "tttttttt"
+WIN_LATE = 1
+SC_SPLIT = (7,)
+GATE = 4
+ACC_BANK = (3, 0, 3, 3, 3, 3, 3, 3)
+IL = "sg"
+MEMSETS = "vgvgg"
+SCALE_QUEUE = "aaaass"
+H_BUFS = 7
+Z_BUFS = 5
+XS_BUFS = 2
+CUR_BUFS = 7
+RW_BUFS = 2
+TURN_BUFS = 2
+SZ_BANKS = 2
+XN_BANKS = 2
+HN_BANKS = 2
+TURN_BANKS = 2
+SPLIT = (0, 5, 6, 7)
+STAGES = ((4, 0), (5, 0), (0, -2), (1, -2), (2, -2), (3, -2))
 
 
 def load_scale_rows(queue, planes, scales):
@@ -39,7 +65,7 @@ def tile_list_tgn_mgu_kernel(
     nc = tc.nc
     with ExitStack() as ctx:
         keep = ctx.enter_context(tc.tile_pool(name="keep", bufs=1))
-        hpool = ctx.enter_context(tc.tile_pool(name="hpool", bufs=4))
+        hpool = ctx.enter_context(tc.tile_pool(name="hpool", bufs=H_BUFS))
         work = ctx.enter_context(tc.tile_pool(name="work", bufs=2))
         psum = ctx.enter_context(tc.psum_pool(name="psum", bufs=1))
 
@@ -48,47 +74,87 @@ def tile_list_tgn_mgu_kernel(
 
         tab_planes = keep.tile([P, 2, T // 4], I32, name="tab_planes", align_bytes=64)
         w_planes = keep.tile([P, 6, N // 4], I32, name="w_planes", align_bytes=64)
-        vec_rows = keep.tile([P, P], F32, name="vec_rows")
-        nc.vector.memset(tab_planes[:], 0)
-        nc.vector.memset(w_planes[:], 0)
-        nc.vector.memset(vec_rows[:], 0.0)
-
-        table = keep.tile([P, T], I32, name="table", align_bytes=64)
-        nc.sync.dma_start(out=table[:], in_=tab_words[0].rearrange("p t b -> p (t b)").bitcast(I32))
-        load_scale_rows(nc.sync, tab_planes, tab_scales)
-
-        x_raw = [keep.tile([P, 4, HALF], F32, name=f"x_raw{h}") for h in range(HALVES)]
-        x_rows = x.rearrange("(p i) j -> p i j", i=4)
-        nc.sync.dma_start(out=x_raw[0][:], in_=x_rows[:, :, 0:HALF])
-
-        load_scale_rows(nc.scalar, w_planes[:, 0:1, :], wz_scales)
-        load_scale_rows(nc.scalar, w_planes[:, 1:3, :], uz_scales)
-        load_scale_rows(nc.scalar, w_planes[:, 3:4, :], wn_scales)
-        load_scale_rows(nc.scalar, w_planes[:, 4:6, :], un_scales)
-        nc.scalar.dma_start(out=vec_rows[0:TILES, :], in_=bz.rearrange("(c p) -> c p", p=P))
-        nc.scalar.dma_start(out=vec_rows[TILES : 2 * TILES, :], in_=bn.rearrange("(c p) -> c p", p=P))
-
-        wz = keep.tile([P, N], I32, name="wz", align_bytes=64)
-        wn = keep.tile([P, N], I32, name="wn", align_bytes=64)
-        uz = keep.tile([P, 2, N // 2], I32, name="uz", align_bytes=64)
-        un = keep.tile([P, 2, N // 2], I32, name="un", align_bytes=64)
-        nc.sync.dma_start(out=wz[:], in_=wz_words[0].rearrange("p n b -> p (n b)").bitcast(I32))
-        nc.sync.dma_start(out=uz[:], in_=uz_words.rearrange("a p n -> p a n").bitcast(I32))
-        nc.sync.dma_start(out=un[:], in_=un_words.rearrange("a p n -> p a n").bitcast(I32))
-        nc.sync.dma_start(out=wn[:], in_=wn_words[0].rearrange("p n b -> p (n b)").bitcast(I32))
-        nc.sync.dma_start(out=x_raw[1][:], in_=x_rows[:, :, HALF:J])
-        weight = keep.tile([P, J], F32, name="weight")
-
-        windows = [keep.tile([P, T], F32, name=f"window{i}") for i in range(WINDOWS)]
-        for win in windows:
-            nc.vector.memset(win[:], 0.0)
-
+        bias_rows = keep.tile([P, P], F32, name="bias_rows")
+        zero = [nc.vector if e == "v" else nc.gpsimd for e in MEMSETS]
+        zero[2].memset(bias_rows[:], 0.0)
+        zero[0].memset(tab_planes[:], 0)
+        zero[1].memset(w_planes[:], 0)
         ident = keep.tile([P, P], F32, name="ident")
         make_identity(nc, ident[:])
-        vec_ps = psum.tile([P, P], F32, name="vec_ps", tag="sz0")
-        nc.tensor.transpose(vec_ps[:], vec_rows[:], ident[:])
+        windows = [keep.tile([P, T], F32, name=f"window{i}") for i in range(WINDOWS)]
+        if not WIN_LATE:
+            for win in windows:
+                nc.gpsimd.memset(win[:], 0.0)
+
+        x_raw = {}
+        x_rows = x.rearrange("(p i) j -> p i j", i=4)
+        wz, wn, uz, un = {}, {}, {}, {}
+        queue = [{"s": nc.sync, "a": nc.scalar, "g": nc.gpsimd}[q] for q in SCALE_QUEUE]
+        h_all = {}
+        for what in LOADS:
+            if what == "tabs":
+                load_scale_rows(queue[5], tab_planes, tab_scales)
+            elif what == "table":
+                table = hpool.tile([P, T], I32, name="table", tag="big", align_bytes=64)
+                nc.sync.dma_start(out=table[:], in_=tab_words[0].rearrange("p t b -> p (t b)").bitcast(I32))
+            elif what == "x0":
+                x_raw[0] = hpool.tile([P, 4, HALF], F32, name="x_raw0", tag="big", align_bytes=64)
+                nc.sync.dma_start(out=x_raw[0][:], in_=x_rows[:, :, 0:HALF])
+            elif what == "x1":
+                x_raw[1] = hpool.tile([P, 4, HALF], F32, name="x_raw1", tag="big", align_bytes=64)
+                nc.sync.dma_start(out=x_raw[1][:], in_=x_rows[:, :, HALF:J])
+            elif what == "wzs":
+                load_scale_rows(queue[0], w_planes[:, 0:1, :], wz_scales)
+            elif what == "uzs":
+                load_scale_rows(queue[1], w_planes[:, 1:3, :], uz_scales)
+            elif what == "wns":
+                load_scale_rows(queue[2], w_planes[:, 3:4, :], wn_scales)
+            elif what == "uns":
+                load_scale_rows(queue[3], w_planes[:, 4:6, :], un_scales)
+            elif what[0] in "zn":
+                k = int(what[1:])
+                lo, hi = CHUNKS[k] * P, CHUNKS[k + 1] * P
+                if lo == hi:
+                    continue
+                w_hbm, u_hbm, w_sb, u_sb = (
+                    (wz_words, uz_words, wz, uz) if what[0] == "z" else (wn_words, un_words, wn, un)
+                )
+                u_tile = keep.tile([P, 2, (hi - lo) // 2], I32, name=f"u{what}", align_bytes=64)
+                w_tile = keep.tile([P, hi - lo], I32, name=f"w{what}", align_bytes=64)
+                nc.sync.dma_start(
+                    out=u_tile[:], in_=u_hbm[:, :, 2 * lo : 2 * hi].rearrange("a p n -> p a n").bitcast(I32)
+                )
+                nc.sync.dma_start(
+                    out=w_tile[:], in_=w_hbm[0].rearrange("p n b -> p (n b)")[:, 4 * lo : 4 * hi].bitcast(I32)
+                )
+                for c in range(CHUNKS[k], CHUNKS[k + 1]):
+                    at = c * P - lo
+                    w_sb[c] = w_tile[:, at : at + P]
+                    u_sb[c] = [u_tile[:, a, at // 2 : (at + P) // 2] for a in range(2)]
+            elif what == "bias":
+                queue[4].dma_start(out=bias_rows[0:TILES, :], in_=bz.rearrange("(c p) -> c p", p=P))
+                queue[4].dma_start(out=bias_rows[TILES : 2 * TILES, :], in_=bn.rearrange("(c p) -> c p", p=P))
+            elif what == "W":
+                if FINAL != "tttttttt":
+                    weight_all = keep.tile([P, J], F32, name="weight_all")
+                    nc.sync.dma_start(out=weight_all[:], in_=wgo)
+            elif what == "w" and "t" not in FINAL:
+                pass
+            elif what == "w":
+                weight_rows = hpool.tile([P, P], F32, name="weight_rows", tag="big", align_bytes=64)
+                nc.sync.dma_start(out=weight_rows[:], in_=wgo[0:16, :].rearrange("r (c p) -> (r c) p", p=P))
+            else:
+                c = int(what[1:])
+                h_all[c] = hpool.tile([P, T], F32, name="h_all", tag="big", align_bytes=64)
+                nc.sync.dma_start(out=h_all[c][:], in_=hT[c * P : (c + 1) * P, :])
+
+        if WIN_LATE:
+            for i in range(WINDOWS):
+                zero[3 + i].memset(windows[i][:], 0.0)
+        bias_ps = psum.tile([P, P], F32, name="bias_ps", tag="bank30")
+        nc.tensor.transpose(bias_ps[:], bias_rows[:], ident[:])
         bias = keep.tile([P, 2 * TILES], F32, name="bias")
-        nc.scalar.copy(out=bias[:], in_=vec_ps[:, 0 : 2 * TILES])
+        nc.scalar.copy(out=bias[:], in_=bias_ps[:, 0 : 2 * TILES])
 
         picked = keep.tile([P, J], U32, name="picked", align_bytes=64)
         v_codes = keep.tile([P, HALVES, 2, 2 * HALF], U8, name="v_codes", align_bytes=64)
@@ -99,12 +165,17 @@ def tile_list_tgn_mgu_kernel(
         for h in range(HALVES):
             cols = slice(h * HALF, (h + 1) * HALF)
             part = offsets[:, h * HALF // 16 : (h + 1) * HALF // 16]
-            nc.scalar.copy(out=x_bf[:, h, :, :], in_=x_raw[h][:].rearrange("p i j -> p j i"))
-            nc.vector.tensor_copy(out=picked[:, cols], in_=table[:].bitcast(U32).indirect(part))
+            if IL[h] == "s":
+                nc.scalar.copy(out=x_bf[:, h, :, :], in_=x_raw[h][:].rearrange("p i j -> p j i"))
+            else:
+                (nc.vector if IL[h] == "v" else nc.gpsimd).tensor_copy(
+                    out=x_bf[:, h, :, :], in_=x_raw[h][:].rearrange("p i j -> p j i")
+                )
             for a in range(2):
                 nc.vector.tensor_copy(
                     out=v_scales[:, h, a, :], in_=tab_planes[:, a, :].bitcast(U8).indirect(part)
                 )
+            nc.vector.tensor_copy(out=picked[:, cols], in_=table[:].bitcast(U32).indirect(part))
             nc.vector.tensor_copy(
                 out=v_codes[:, h, :, :].bitcast(U16),
                 in_=picked[:, cols].bitcast(U16).rearrange("p (j d) -> p d j", d=2),
@@ -120,7 +191,7 @@ def tile_list_tgn_mgu_kernel(
         def x_pass(bank, words, plane, c, h, start, stop):
             nc.tensor.matmul_mx(
                 out=bank[:],
-                lhsT=words[:, c * P : (c + 1) * P].bitcast(FP8X4),
+                lhsT=words[c].bitcast(FP8X4),
                 lhsT_scale=w_scale[:, plane, c * P : (c + 1) * P],
                 rhs=x_codes[:, h * HALF : (h + 1) * HALF].bitcast(FP8X4),
                 rhs_scale=x_scales[:, h * HALF : (h + 1) * HALF],
@@ -131,7 +202,7 @@ def tile_list_tgn_mgu_kernel(
         def v_pass(bank, words, plane, a, c, h, start, stop):
             nc.tensor.matmul_mx(
                 out=bank[:],
-                lhsT=words[:, a, :].bitcast(U8)[:, 2 * c * P : 2 * (c + 1) * P].bitcast(FP4X4),
+                lhsT=words[c][a].bitcast(U8).bitcast(FP4X4),
                 lhsT_scale=w_scale[:, plane + a, c * P : (c + 1) * P],
                 rhs=v_codes[:, h, a, :].bitcast(FP4X4),
                 rhs_scale=v_scales[:, h, a, :],
@@ -139,48 +210,125 @@ def tile_list_tgn_mgu_kernel(
                 stop=stop,
             )
 
-        for c in range(TILES):
-            rows = slice(c * P, (c + 1) * P)
-            h_all = hpool.tile([P, T], F32, name="h_all")
-            nc.sync.dma_start(out=h_all[:], in_=hT[rows, :])
-            if c == 0:
-                nc.sync.dma_start(out=weight[:], in_=wgo)
+        z, xs, cur, hg, rw = {}, {}, {}, {}, {}
+        weight = keep.tile([P, J // P], F32, name="weight")
 
-            z = work.tile([P, J], F32, name="z", bufs=3)
-            u = work.tile([P, J], F32, name="u")
-            t = work.tile([P, J], F32, name="t")
-            cd = work.tile([P, J], F32, name="cd")
-            xn = []
+        def spans(c):
+            return [slice(h * HALF, (h + 1) * HALF) for h in range(HALVES)] if c in SPLIT else [slice(0, J)]
+
+        def products(c):
+            z[c] = work.tile([P, J], F32, name="z", bufs=Z_BUFS)
+            if c not in T_ON_V:
+                xs[c] = work.tile([P, J], F32, name="xs", bufs=XS_BUFS)
+            banks = []
+            cur[c] = work.tile([P, J], F32, name="cur", bufs=CUR_BUFS)
+            prod = work.tile([P, J], F32, name="prod", tag="spare", bufs=1) if c == GATE else cur[c]
             for h in range(HALVES):
                 cols = slice(h * HALF, (h + 1) * HALF)
                 unit = HALVES * c + h
-                sz = psum.tile([P, HALF], F32, name="sz", tag=f"sz{unit % 2}")
+                sz = psum.tile([P, HALF], F32, name="sz", tag=f"bank0{h}")
                 v_pass(sz, uz, 1, 0, c, h, True, False)
                 v_pass(sz, uz, 1, 1, c, h, False, False)
                 x_pass(sz, wz, 0, c, h, False, True)
-                hn = psum.tile([P, HALF], F32, name="hn", tag=f"hn{unit % 3}")
+                hn = psum.tile([P, HALF], F32, name="hn", tag=f"bank1{h}")
                 v_pass(hn, un, 4, 0, c, h, True, False)
                 v_pass(hn, un, 4, 1, c, h, False, True)
-                xb = psum.tile([P, HALF], F32, name="xb", tag=f"xn{unit % 3}")
+                xb = psum.tile([P, HALF], F32, name="xb", tag=f"bank2{h}")
                 x_pass(xb, wn, 3, c, h, True, True)
-                xn.append(xb)
-                nc.scalar.activation(out=z[:, cols], in_=sz[:], func=ACT.Sigmoid, bias=bias[:, c : c + 1])
-                nc.vector.tensor_tensor(out=u[:, cols], in0=z[:, cols], in1=hn[:], op=ALU.mult)
-            for h in range(HALVES):
-                cols = slice(h * HALF, (h + 1) * HALF)
-                nc.vector.tensor_tensor(out=t[:, cols], in0=u[:, cols], in1=xn[h][:], op=ALU.add)
-            nc.scalar.activation(out=cd[:], in_=t[:], func=ACT.Tanh, bias=bias[:, TILES + c : TILES + c + 1])
+                nc.scalar.activation(out=z[c][:, cols], in_=sz[:], func=ACT.Sigmoid, bias=bias[:, c : c + 1])
+                banks.append(xb)
+                if c not in T_ON_V:
+                    nc.scalar.activation(
+                        out=xs[c][:, cols], in_=xb[:], func=ACT.Identity, bias=bias[:, TILES + c : TILES + c + 1]
+                    )
+                if c in U_ON_GPSIMD and c not in T_ON_V:
+                    nc.scalar.copy(out=cur[c][:, cols], in_=hn[:])
+                else:
+                    nc.vector.tensor_tensor(out=prod[:, cols], in0=z[c][:, cols], in1=hn[:], op=ALU.mult)
+                if c in T_ON_V and XN_BANKS == 1:
+                    nc.vector.tensor_tensor(out=cur[c][:, cols], in0=cur[c][:, cols], in1=xb[:], op=ALU.add)
+            if c in T_ON_V and XN_BANKS > 1:
+                for h in range(HALVES):
+                    cols = slice(h * HALF, (h + 1) * HALF)
+                    nc.vector.tensor_tensor(out=cur[c][:, cols], in0=prod[:, cols], in1=banks[h][:], op=ALU.add)
 
-            hg = work.tile([P, J], F32, name="hg", bufs=6)
-            nc.vector.tensor_copy(out=hg[:], in_=h_all[:].indirect(offsets[:]))
-            d = work.tile([P, J], F32, name="d")
-            e = work.tile([P, J], F32, name="e")
-            r = work.tile([P, J], F32, name="r")
-            rw = work.tile([P, J], F32, name="rw")
-            nc.gpsimd.tensor_tensor(out=d[:], in0=cd[:], in1=hg[:], op=ALU.subtract)
-            nc.gpsimd.tensor_tensor(out=e[:], in0=d[:], in1=z[:], op=ALU.mult)
-            nc.gpsimd.tensor_tensor(out=r[:], in0=e[:], in1=hg[:], op=ALU.add)
-            nc.gpsimd.tensor_tensor(out=rw[:], in0=r[:], in1=weight[:], op=ALU.mult)
+        def gather(c):
+            hg[c] = work.tile([P, J], F32, name="hg", bufs=TILES)
+            nc.vector.tensor_copy(out=hg[c][:], in_=h_all[c][:].indirect(offsets[:]))
+
+        def candidate(c):
+            for s in spans(c):
+                if c in T_ON_V:
+                    nc.scalar.activation(
+                        out=cur[c][:, s], in_=cur[c][:, s], func=ACT.Tanh, bias=bias[:, TILES + c : TILES + c + 1]
+                    )
+                    continue
+                if c in U_ON_GPSIMD:
+                    nc.gpsimd.tensor_tensor(out=cur[c][:, s], in0=cur[c][:, s], in1=z[c][:, s], op=ALU.mult)
+                nc.gpsimd.tensor_tensor(out=cur[c][:, s], in0=cur[c][:, s], in1=xs[c][:, s], op=ALU.add)
+                nc.scalar.activation(out=cur[c][:, s], in_=cur[c][:, s], func=ACT.Tanh)
+
+        def change(c):
+            eng = nc.vector if c in DE_ON_V else nc.gpsimd
+            for s in spans(c):
+                eng.tensor_tensor(out=cur[c][:, s], in0=cur[c][:, s], in1=hg[c][:, s], op=ALU.subtract)
+                if c in SPLIT_MUL:
+                    eng.tensor_tensor(out=cur[c][:, s], in0=cur[c][:, s], in1=z[c][:, s], op=ALU.mult)
+            if c not in SPLIT_MUL:
+                eng.tensor_tensor(out=cur[c][:], in0=cur[c][:], in1=z[c][:], op=ALU.mult)
+
+        def add_and_weigh(c):
+            if FINAL[c] != "t":
+                eng = nc.vector if FINAL[c] in "vV" else nc.gpsimd
+                for s in spans(c) if c in SPLIT_MUL else [slice(0, J)]:
+                    eng.tensor_tensor(out=cur[c][:, s], in0=cur[c][:, s], in1=hg[c][:, s], op=ALU.add)
+                    if FINAL[c] in "gV":
+                        eng.tensor_tensor(out=cur[c][:, s], in0=cur[c][:, s], in1=weight_all[:, s], op=ALU.mult)
+                return
+            if c == FINAL.index("t"):
+                weight_ps = psum.tile([P, P], F32, name="weight_ps", tag="bank31")
+                nc.tensor.transpose(weight_ps[:], weight_rows[:], ident[:])
+                nc.scalar.copy(out=weight[:], in_=weight_ps[:, 0 : J // P])
+            rw[c] = work.tile([P, J], F32, name="first", tag="spare", bufs=1) if c == 0 and GATE >= 0 else cur[c]
+            turned = work.tile([P, J], F32, name="turned", bufs=TURN_BUFS)
+            for h in range(HALVES):
+                acc = psum.tile([P, HALF], F32, name="acc", tag=f"bank{ACC_BANK[c]}{h}")
+                for b in range(4):
+                    blk = slice(h * HALF + b * P, h * HALF + (b + 1) * P)
+                    for src, first in ((hg[c], True), (cur[c], False)):
+                        nc.tensor.matmul(
+                            acc[:, b * P : (b + 1) * P], lhsT=src[:, blk], rhs=ident[:],
+                            is_transpose=True, start=first, stop=not first,
+                        )
+                for b in range(4):
+                    blk = slice(h * HALF + b * P, h * HALF + (b + 1) * P)
+                    nc.scalar.activation(
+                        out=turned[:, blk], in_=acc[:, b * P : (b + 1) * P], func=ACT.Copy,
+                        scale=weight[:, 4 * h + b : 4 * h + b + 1],
+                    )
+            for h in range(HALVES):
+                back = psum.tile([P, HALF], F32, name="back", tag=f"bank{ACC_BANK[c]}{h}")
+                for b in range(4):
+                    blk = slice(h * HALF + b * P, h * HALF + (b + 1) * P)
+                    nc.tensor.transpose(back[:, b * P : (b + 1) * P], turned[:, blk], ident[:])
+                nc.scalar.copy(out=rw[c][:, h * HALF : (h + 1) * HALF], in_=back[:])
+
+        def scatter(c):
             win = windows[c % WINDOWS]
-            nc.vector.tensor_copy(out=win[:].indirect(offsets[:]), in_=rw[:])
-            nc.sync.dma_start(out=out[rows, :], in_=win[:])
+            for s in [slice(0, HALF), slice(HALF, J)] if c in SC_SPLIT else [slice(0, J)]:
+                places = win[:].indirect(offsets[:, s.start // 16 : s.stop // 16])
+                if FINAL[c] in "fv":
+                    nc.vector.tensor_tensor(out=places, in0=cur[c][:, s], in1=weight_all[:, s], op=ALU.mult)
+                else:
+                    nc.vector.tensor_copy(out=places, in_=rw.get(c, cur[c])[:, s])
+            nc.sync.dma_start(out=out[c * P : (c + 1) * P, :], in_=win[:])
+
+        stage_list = (products, candidate, gather, change, add_and_weigh, scatter)
+        for c in range(GATE + 1):
+            for stage in stage_list[:4]:
+                stage(c)
+        for step in range(TILES + 6):
+            for stage, lag in STAGES:
+                c = step - lag
+                if 0 <= c < TILES and (stage >= 4 or c > GATE):
+                    stage_list[stage](c)

@@ -33,8 +33,8 @@ WIN_LATE = 1
 SC_SPLIT = (7,)
 GATE = 4
 ACC_BANK = (3, 0, 3, 3, 3, 3, 3, 3)
-IL = "sg"
-MEMSETS = "vgvgg"
+IL = "ss"
+MEMSETS = "vgvggg"
 SCALE_QUEUE = "aaaass"
 H_BUFS = 7
 Z_BUFS = 5

@@ -21,10 +21,10 @@ P = 128
 HALF = 512
 HALVES = J // HALF
 TILES = N // P
-WINDOWS = 2
+WINDOWS = 3
 U_ON_GPSIMD = (5, 6, 7)
-LOADS = ("bias", "tabs", "table", "x0", "uzs", "wzs", "uns", "wns", "x1", "h0", "z0", "n0", "h1", "h2", "z1", "n1", "z2", "n2", "w", "h3", "h4", "h5", "h6", "h7", "W")
-CHUNKS = (0, 2, 8, 8)
+LOADS = ("bias", "tabs", "table", "x0", "uzs", "wzs", "uns", "wns", "x1", "h0", "z0", "n0", "h1", "z1", "n1", "h2", "z2", "n2", "h3", "w", "h4", "h5", "h6", "h7", "W")
+CHUNKS = (0, 2, 5, 8)
 SPLIT_MUL = (0, 7)
 T_ON_V = (0, 1, 2, 3, 4)
 DE_ON_V = ()
@@ -32,9 +32,10 @@ FINAL = "tttttttt"
 WIN_LATE = 1
 SC_SPLIT = (7,)
 GATE = 4
+STORE_SPLIT = 2
 ACC_BANK = (3, 0, 3, 3, 3, 3, 3, 3)
 IL = "ss"
-MEMSETS = "vgvggg"
+MEMSETS = "vgvvvg"
 SCALE_QUEUE = "aaaass"
 H_BUFS = 7
 Z_BUFS = 5
@@ -321,7 +322,9 @@ def tile_list_tgn_mgu_kernel(
                     nc.vector.tensor_tensor(out=places, in0=cur[c][:, s], in1=weight_all[:, s], op=ALU.mult)
                 else:
                     nc.vector.tensor_copy(out=places, in_=rw.get(c, cur[c])[:, s])
-            nc.sync.dma_start(out=out[c * P : (c + 1) * P, :], in_=win[:])
+            for k in range(STORE_SPLIT):
+                part = slice(k * T // STORE_SPLIT, (k + 1) * T // STORE_SPLIT)
+                nc.sync.dma_start(out=out[c * P : (c + 1) * P, part], in_=win[:, part])
 
         stage_list = (products, candidate, gather, change, add_and_weigh, scatter)
         for c in range(GATE + 1):

from contextlib import ExitStack

import concourse.mybir as mybir
from concourse.masks import make_identity

K, M, N, T, J = 512, 1024, 1024, 2048, 1024
FLOPS = 2 * J * N * (2 * K + 2 * M)

F32 = mybir.dt.float32
BF16 = mybir.dt.bfloat16
I32 = mybir.dt.int32
U32 = mybir.dt.uint32
U16 = mybir.dt.uint16
U8 = mybir.dt.uint8
FP8X4 = mybir.dt.float8_e4m3fn_x4
FP4X4 = mybir.dt.float4_e2m1fn_x4
ACT = mybir.ActivationFunctionType
ALU = mybir.AluOpType

P = 128
HALF = 512
HALVES = J // HALF
TILES = N // P
WINDOWS = 3
U_ON_GPSIMD = (5, 6, 7)
LOADS = ("bias", "tabs", "table", "x0", "uzs", "wzs", "uns", "wns", "x1", "h0", "z0", "n0", "h1", "z1", "n1", "h2", "z2", "n2", "h3", "w", "h4", "h5", "h6", "h7", "W")
CHUNKS = (0, 2, 5, 8)
SPLIT_MUL = (0, 7)
T_ON_V = (0, 1, 2, 3, 4)
DE_ON_V = ()
FINAL = "tttttttt"
WIN_LATE = 1
SC_SPLIT = (7,)
GATE = 4
STORE_SPLIT = 2
ACC_BANK = (3, 0, 3, 3, 3, 3, 3, 3)
IL = "ss"
MEMSETS = "vgvvvg"
SCALE_QUEUE = "aaaass"
H_BUFS = 7
Z_BUFS = 5
XS_BUFS = 2
CUR_BUFS = 7
RW_BUFS = 2
TURN_BUFS = 2
SZ_BANKS = 2
XN_BANKS = 2
HN_BANKS = 2
TURN_BANKS = 2
SPLIT = (0, 5, 6, 7)
STAGES = ((4, 0), (5, 0), (0, -2), (1, -2), (2, -2), (3, -2))


def load_scale_rows(queue, planes, scales):
    for q in range(4):
        queue.dma_start(
            out=planes[32 * q : 32 * q + 4, :, :],
            in_=scales[:, 4 * q : 4 * q + 4, :].rearrange("a r n -> r a n").bitcast(I32),
        )


def tile_list_tgn_mgu_kernel(
    tc, x, tab_words, tab_scales, wz_words, wz_scales, uz_words, uz_scales,
    wn_words, wn_scales, un_words, un_scales, bz, bn, hT, wgo, offs, out,
):
    nc = tc.nc
    with ExitStack() as ctx:
        keep = ctx.enter_context(tc.tile_pool(name="keep", bufs=1))
        hpool = ctx.enter_context(tc.tile_pool(name="hpool", bufs=H_BUFS))
        work = ctx.enter_context(tc.tile_pool(name="work", bufs=2))
        psum = ctx.enter_context(tc.psum_pool(name="psum", bufs=1))

        offsets = keep.tile([P, J // 16], U16, name="offsets")
        nc.sync.dma_start(offsets[:], offs)

        tab_planes = keep.tile([P, 2, T // 4], I32, name="tab_planes", align_bytes=64)
        w_planes = keep.tile([P, 6, N // 4], I32, name="w_planes", align_bytes=64)
        bias_rows = keep.tile([P, P], F32, name="bias_rows")
        zero = [nc.vector if e == "v" else nc.gpsimd for e in MEMSETS]
        zero[2].memset(bias_rows[:], 0.0)
        zero[0].memset(tab_planes[:], 0)
        zero[1].memset(w_planes[:], 0)
        ident = keep.tile([P, P], F32, name="ident")
        make_identity(nc, ident[:])
        windows = [keep.tile([P, T], F32, name=f"window{i}") for i in range(WINDOWS)]
        if not WIN_LATE:
            for win in windows:
                nc.gpsimd.memset(win[:], 0.0)

        x_raw = {}
        x_rows = x.rearrange("(p i) j -> p i j", i=4)
        wz, wn, uz, un = {}, {}, {}, {}
        queue = [{"s": nc.sync, "a": nc.scalar, "g": nc.gpsimd}[q] for q in SCALE_QUEUE]
        h_all = {}
        for what in LOADS:
            if what == "tabs":
                load_scale_rows(queue[5], tab_planes, tab_scales)
            elif what == "table":
                table = hpool.tile([P, T], I32, name="table", tag="big", align_bytes=64)
                nc.sync.dma_start(out=table[:], in_=tab_words[0].rearrange("p t b -> p (t b)").bitcast(I32))
            elif what == "x0":
                x_raw[0] = hpool.tile([P, 4, HALF], F32, name="x_raw0", tag="big", align_bytes=64)
                nc.sync.dma_start(out=x_raw[0][:], in_=x_rows[:, :, 0:HALF])
            elif what == "x1":
                x_raw[1] = hpool.tile([P, 4, HALF], F32, name="x_raw1", tag="big", align_bytes=64)
                nc.sync.dma_start(out=x_raw[1][:], in_=x_rows[:, :, HALF:J])
            elif what == "wzs":
                load_scale_rows(queue[0], w_planes[:, 0:1, :], wz_scales)
            elif what == "uzs":
                load_scale_rows(queue[1], w_planes[:, 1:3, :], uz_scales)
            elif what == "wns":
                load_scale_rows(queue[2], w_planes[:, 3:4, :], wn_scales)
            elif what == "uns":
                load_scale_rows(queue[3], w_planes[:, 4:6, :], un_scales)
            elif what[0] in "zn":
                k = int(what[1:])
                lo, hi = CHUNKS[k] * P, CHUNKS[k + 1] * P
                if lo == hi:
                    continue
                w_hbm, u_hbm, w_sb, u_sb = (
                    (wz_words, uz_words, wz, uz) if what[0] == "z" else (wn_words, un_words, wn, un)
                )
                u_tile = keep.tile([P, 2, (hi - lo) // 2], I32, name=f"u{what}", align_bytes=64)
                w_tile = keep.tile([P, hi - lo], I32, name=f"w{what}", align_bytes=64)
                nc.sync.dma_start(
                    out=u_tile[:], in_=u_hbm[:, :, 2 * lo : 2 * hi].rearrange("a p n -> p a n").bitcast(I32)
                )
                nc.sync.dma_start(
                    out=w_tile[:], in_=w_hbm[0].rearrange("p n b -> p (n b)")[:, 4 * lo : 4 * hi].bitcast(I32)
                )
                for c in range(CHUNKS[k], CHUNKS[k + 1]):
                    at = c * P - lo
                    w_sb[c] = w_tile[:, at : at + P]
                    u_sb[c] = [u_tile[:, a, at // 2 : (at + P) // 2] for a in range(2)]
            elif what == "bias":
                queue[4].dma_start(out=bias_rows[0:TILES, :], in_=bz.rearrange("(c p) -> c p", p=P))
                queue[4].dma_start(out=bias_rows[TILES : 2 * TILES, :], in_=bn.rearrange("(c p) -> c p", p=P))
            elif what == "W":
                if FINAL != "tttttttt":
                    weight_all = keep.tile([P, J], F32, name="weight_all")
                    nc.sync.dma_start(out=weight_all[:], in_=wgo)
            elif what == "w" and "t" not in FINAL:
                pass
            elif what == "w":
                weight_rows = hpool.tile([P, P], F32, name="weight_rows", tag="big", align_bytes=64)
                nc.sync.dma_start(out=weight_rows[:], in_=wgo[0:16, :].rearrange("r (c p) -> (r c) p", p=P))
            else:
                c = int(what[1:])
                h_all[c] = hpool.tile([P, T], F32, name="h_all", tag="big", align_bytes=64)
                nc.sync.dma_start(out=h_all[c][:], in_=hT[c * P : (c + 1) * P, :])

        if WIN_LATE:
            for i in range(WINDOWS):
                zero[3 + i].memset(windows[i][:], 0.0)
        bias_ps = psum.tile([P, P], F32, name="bias_ps", tag="bank30")
        nc.tensor.transpose(bias_ps[:], bias_rows[:], ident[:])
        bias = keep.tile([P, 2 * TILES], F32, name="bias")
        nc.scalar.copy(out=bias[:], in_=bias_ps[:, 0 : 2 * TILES])

        picked = keep.tile([P, J], U32, name="picked", align_bytes=64)
        v_codes = keep.tile([P, HALVES, 2, 2 * HALF], U8, name="v_codes", align_bytes=64)
        v_scales = keep.tile([P, HALVES, 2, HALF], U8, name="v_scales", align_bytes=64)
        x_bf = keep.tile([P, HALVES, HALF, 4], BF16, name="x_bf", align_bytes=64)
        x_codes = keep.tile([P, J], U32, name="x_codes", align_bytes=64)
        x_scales = keep.tile([P, J], U8, name="x_scales", align_bytes=64)
        for h in range(HALVES):
            cols = slice(h * HALF, (h + 1) * HALF)
            part = offsets[:, h * HALF // 16 : (h + 1) * HALF // 16]
            if IL[h] == "s":
                nc.scalar.copy(out=x_bf[:, h, :, :], in_=x_raw[h][:].rearrange("p i j -> p j i"))
            else:
                (nc.vector if IL[h] == "v" else nc.gpsimd).tensor_copy(
                    out=x_bf[:, h, :, :], in_=x_raw[h][:].rearrange("p i j -> p j i")
                )
            for a in range(2):
                nc.vector.tensor_copy(
                    out=v_scales[:, h, a, :], in_=tab_planes[:, a, :].bitcast(U8).indirect(part)
                )
            nc.vector.tensor_copy(out=picked[:, cols], in_=table[:].bitcast(U32).indirect(part))
            nc.vector.tensor_copy(
                out=v_codes[:, h, :, :].bitcast(U16),
                in_=picked[:, cols].bitcast(U16).rearrange("p (j d) -> p d j", d=2),
            )
            nc.vector.quantize_mx(
                out=x_codes[:, cols].bitcast(FP8X4),
                scales=x_scales[:, cols],
                in_=x_bf[:, h, :, :].rearrange("p j i -> p (j i)"),
            )

        w_scale = w_planes[:].bitcast(U8)

        def x_pass(bank, words, plane, c, h, start, stop):
            nc.tensor.matmul_mx(
                out=bank[:],
                lhsT=words[c].bitcast(FP8X4),
                lhsT_scale=w_scale[:, plane, c * P : (c + 1) * P],
                rhs=x_codes[:, h * HALF : (h + 1) * HALF].bitcast(FP8X4),
                rhs_scale=x_scales[:, h * HALF : (h + 1) * HALF],
                start=start,
                stop=stop,
            )

        def v_pass(bank, words, plane, a, c, h, start, stop):
            nc.tensor.matmul_mx(
                out=bank[:],
                lhsT=words[c][a].bitcast(U8).bitcast(FP4X4),
                lhsT_scale=w_scale[:, plane + a, c * P : (c + 1) * P],
                rhs=v_codes[:, h, a, :].bitcast(FP4X4),
                rhs_scale=v_scales[:, h, a, :],
                start=start,
                stop=stop,
            )

        z, xs, cur, hg, rw = {}, {}, {}, {}, {}
        weight = keep.tile([P, J // P], F32, name="weight")

        def spans(c):
            return [slice(h * HALF, (h + 1) * HALF) for h in range(HALVES)] if c in SPLIT else [slice(0, J)]

        def products(c):
            z[c] = work.tile([P, J], F32, name="z", bufs=Z_BUFS)
            if c not in T_ON_V:
                xs[c] = work.tile([P, J], F32, name="xs", bufs=XS_BUFS)
            banks = []
            cur[c] = work.tile([P, J], F32, name="cur", bufs=CUR_BUFS)
            prod = work.tile([P, J], F32, name="prod", tag="spare", bufs=1) if c == GATE else cur[c]
            for h in range(HALVES):
                cols = slice(h * HALF, (h + 1) * HALF)
                unit = HALVES * c + h
                sz = psum.tile([P, HALF], F32, name="sz", tag=f"bank0{h}")
                v_pass(sz, uz, 1, 0, c, h, True, False)
                v_pass(sz, uz, 1, 1, c, h, False, False)
                x_pass(sz, wz, 0, c, h, False, True)
                hn = psum.tile([P, HALF], F32, name="hn", tag=f"bank1{h}")
                v_pass(hn, un, 4, 0, c, h, True, False)
                v_pass(hn, un, 4, 1, c, h, False, True)
                xb = psum.tile([P, HALF], F32, name="xb", tag=f"bank2{h}")
                x_pass(xb, wn, 3, c, h, True, True)
                nc.scalar.activation(out=z[c][:, cols], in_=sz[:], func=ACT.Sigmoid, bias=bias[:, c : c + 1])
                banks.append(xb)
                if c not in T_ON_V:
                    nc.scalar.activation(
                        out=xs[c][:, cols], in_=xb[:], func=ACT.Identity, bias=bias[:, TILES + c : TILES + c + 1]
                    )
                if c in U_ON_GPSIMD and c not in T_ON_V:
                    nc.scalar.copy(out=cur[c][:, cols], in_=hn[:])
                else:
                    nc.vector.tensor_tensor(out=prod[:, cols], in0=z[c][:, cols], in1=hn[:], op=ALU.mult)
                if c in T_ON_V and XN_BANKS == 1:
                    nc.vector.tensor_tensor(out=cur[c][:, cols], in0=cur[c][:, cols], in1=xb[:], op=ALU.add)
            if c in T_ON_V and XN_BANKS > 1:
                for h in range(HALVES):
                    cols = slice(h * HALF, (h + 1) * HALF)
                    nc.vector.tensor_tensor(out=cur[c][:, cols], in0=prod[:, cols], in1=banks[h][:], op=ALU.add)

        def gather(c):
            hg[c] = work.tile([P, J], F32, name="hg", bufs=TILES)
            nc.vector.tensor_copy(out=hg[c][:], in_=h_all[c][:].indirect(offsets[:]))

        def candidate(c):
            for s in spans(c):
                if c in T_ON_V:
                    nc.scalar.activation(
                        out=cur[c][:, s], in_=cur[c][:, s], func=ACT.Tanh, bias=bias[:, TILES + c : TILES + c + 1]
                    )
                    continue
                if c in U_ON_GPSIMD:
                    nc.gpsimd.tensor_tensor(out=cur[c][:, s], in0=cur[c][:, s], in1=z[c][:, s], op=ALU.mult)
                nc.gpsimd.tensor_tensor(out=cur[c][:, s], in0=cur[c][:, s], in1=xs[c][:, s], op=ALU.add)
                nc.scalar.activation(out=cur[c][:, s], in_=cur[c][:, s], func=ACT.Tanh)

        def change(c):
            eng = nc.vector if c in DE_ON_V else nc.gpsimd
            for s in spans(c):
                eng.tensor_tensor(out=cur[c][:, s], in0=cur[c][:, s], in1=hg[c][:, s], op=ALU.subtract)
                if c in SPLIT_MUL:
                    eng.tensor_tensor(out=cur[c][:, s], in0=cur[c][:, s], in1=z[c][:, s], op=ALU.mult)
            if c not in SPLIT_MUL:
                eng.tensor_tensor(out=cur[c][:], in0=cur[c][:], in1=z[c][:], op=ALU.mult)

        def add_and_weigh(c):
            if FINAL[c] != "t":
                eng = nc.vector if FINAL[c] in "vV" else nc.gpsimd
                for s in spans(c) if c in SPLIT_MUL else [slice(0, J)]:
                    eng.tensor_tensor(out=cur[c][:, s], in0=cur[c][:, s], in1=hg[c][:, s], op=ALU.add)
                    if FINAL[c] in "gV":
                        eng.tensor_tensor(out=cur[c][:, s], in0=cur[c][:, s], in1=weight_all[:, s], op=ALU.mult)
                return
            if c == FINAL.index("t"):
                weight_ps = psum.tile([P, P], F32, name="weight_ps", tag="bank31")
                nc.tensor.transpose(weight_ps[:], weight_rows[:], ident[:])
                nc.scalar.copy(out=weight[:], in_=weight_ps[:, 0 : J // P])
            rw[c] = work.tile([P, J], F32, name="first", tag="spare", bufs=1) if c == 0 and GATE >= 0 else cur[c]
            turned = work.tile([P, J], F32, name="turned", bufs=TURN_BUFS)
            for h in range(HALVES):
                acc = psum.tile([P, HALF], F32, name="acc", tag=f"bank{ACC_BANK[c]}{h}")
                for b in range(4):
                    blk = slice(h * HALF + b * P, h * HALF + (b + 1) * P)
                    for src, first in ((hg[c], True), (cur[c], False)):
                        nc.tensor.matmul(
                            acc[:, b * P : (b + 1) * P], lhsT=src[:, blk], rhs=ident[:],
                            is_transpose=True, start=first, stop=not first,
                        )
                for b in range(4):
                    blk = slice(h * HALF + b * P, h * HALF + (b + 1) * P)
                    nc.scalar.activation(
                        out=turned[:, blk], in_=acc[:, b * P : (b + 1) * P], func=ACT.Copy,
                        scale=weight[:, 4 * h + b : 4 * h + b + 1],
                    )
            for h in range(HALVES):
                back = psum.tile([P, HALF], F32, name="back", tag=f"bank{ACC_BANK[c]}{h}")
                for b in range(4):
                    blk = slice(h * HALF + b * P, h * HALF + (b + 1) * P)
                    nc.tensor.transpose(back[:, b * P : (b + 1) * P], turned[:, blk], ident[:])
                nc.scalar.copy(out=rw[c][:, h * HALF : (h + 1) * HALF], in_=back[:])

        def scatter(c):
            win = windows[c % WINDOWS]
            for s in [slice(0, HALF), slice(HALF, J)] if c in SC_SPLIT else [slice(0, J)]:
                places = win[:].indirect(offsets[:, s.start // 16 : s.stop // 16])
                if FINAL[c] in "fv":
                    nc.vector.tensor_tensor(out=places, in0=cur[c][:, s], in1=weight_all[:, s], op=ALU.mult)
                else:
                    nc.vector.tensor_copy(out=places, in_=rw.get(c, cur[c])[:, s])
            for k in range(STORE_SPLIT):
                part = slice(k * T // STORE_SPLIT, (k + 1) * T // STORE_SPLIT)
                nc.sync.dma_start(out=out[c * P : (c + 1) * P, part], in_=win[:, part])

        stage_list = (products, candidate, gather, change, add_and_weigh, scatter)
        for c in range(GATE + 1):
            for stage in stage_list[:4]:
                stage(c)
        for step in range(TILES + 6):
            for stage, lag in STAGES:
                c = step - lag
                if 0 <= c < TILES and (stage >= 4 or c > GATE):
                    stage_list[stage](c)
